import numpy as np
CORES = [32,160,288,416,80,208,336,464]
N = 8
W, KW, DIL = 128, 3, 8
H = (KW // 2) * DIL
def setup_inputs(rng):
    return {"x": rng.standard_normal((N, 128, W), dtype=np.float32), "w": rng.standard_normal((N, 128, KW * 128), dtype=np.float32)}
def setup_inputs_big(rng):
    d = setup_inputs(rng)
    for k in ("x", "w"): d[k] = (d[k].astype(np.float32) * 1024.0).astype(d[k].dtype)
    return d
def setup_inputs_small(rng):
    d = setup_inputs(rng)
    for k in ("x", "w"): d[k] = (d[k].astype(np.float32) * (1 / 1024.0)).astype(d[k].dtype)
    return d
def setup_inputs_apart(rng):
    d = setup_inputs(rng)
    f = (10.0 ** rng.permutation(np.linspace(-1.5, 1.5, N))).astype(np.float32).reshape(N, 1, 1)
    for k in ("x", "w"): d[k] = (d[k].astype(np.float32) * f).astype(d[k].dtype)
    return d
def reference(x, w):
    X, W_ = x.astype(np.float64), w.astype(np.float64)
    g = np.concatenate(list(X), axis=1)
    p = np.concatenate([g[:, -H:], g, g[:, :H]], axis=1)
    y = np.zeros((N, 128, W))
    for r in range(N):
        for i in range(KW):
            y[r] += W_[r][:, 128 * i:128 * i + 128].T @ p[:, W * r + i * DIL:W * r + i * DIL + W]
    return {"y": y.astype(np.float32 if x.dtype != np.float64 else np.float64)}

@@ -1,0 +1,71 @@
+from concourse.bass import DstId, RemoteDMATransfer
+
+P = 128
+HALO = 8
+ENG = 4
+
+SCRATCH = {
+    "xs": ("sbuf", [P, P], "float32"),
+    "ws": ("sbuf", [P, 3 * P], "float32"),
+    "hL": ("sbuf", [P, HALO], "float32"),
+    "hR": ("sbuf", [P, HALO], "float32"),
+    "ys": ("sbuf", [P, P], "float32"),
+    "acc": ("psum", [P, P], "float32"),
+}
+SEMAPHORES = ["xl", "wl", "sent", "gotL", "gotR", "mm", "cp", "st"]
+
+
+def _links(topo, a, b):
+    if topo.same_plane(a, b):
+        return 1
+    if topo.rack(topo.host(a)) != topo.rack(topo.host(b)) and topo.chip(a) == topo.chip(b):
+        return 1
+    return 2
+
+
+def rank_program(g, core, T, topo):
+    rank = T.rank_of(core)
+    if rank is None:
+        return
+    n = len(T.cores)
+    left, right = T.cores[(rank - 1) % n], T.cores[(rank + 1) % n]
+    S = T.sem
+
+    g.sync.dma_start(T.xs[:], T.x[:]).then_inc(S.xl, 16)
+    g.sync.dma_start(T.ws[:], T.w[:]).then_inc(S.wl, 16)
+
+    both = topo.mask(core, left) & topo.mask(core, right)
+    engines = [e for e in range(16) if (both >> e) & 1]
+    m_left = sum(1 << e for e in engines[0:ENG])
+    m_right = sum(1 << e for e in engines[ENG:2 * ENG])
+    rid_l, pid_l = topo.addr(left, core)
+    rid_r, pid_r = topo.addr(right, core)
+    g.wait_ge(S.xl, 16)
+    g.remote_dma_fused([
+        RemoteDMATransfer(dst_ids=[DstId(rid=rid_l, pnc=pid_l)], dma_engine_mask=m_left, remote_sem=S.gotR,
+                          src=T.xs[:, 0:HALO], dst=T.hR[:]),
+        RemoteDMATransfer(dst_ids=[DstId(rid=rid_r, pnc=pid_r)], dma_engine_mask=m_right, remote_sem=S.gotL,
+                          src=T.xs[:, P - HALO:P], dst=T.hL[:]),
+    ], local_sem=S.sent)
+
+    w0, w1, w2 = T.ws[:, 0:P], T.ws[:, P:2 * P], T.ws[:, 2 * P:3 * P]
+    te = g.tensor
+    te.wait_ge(S.xl, 16)
+    te.wait_ge(S.wl, 16)
+    te.matmul(T.acc[:, 0:P], w1, T.xs[:, 0:P], True, False).then_inc(S.mm, 1)
+    te.matmul(T.acc[:, HALO:P], w0, T.xs[:, 0:P - HALO], False, False).then_inc(S.mm, 1)
+    te.matmul(T.acc[:, 0:P - HALO], w2, T.xs[:, HALO:P], False, False).then_inc(S.mm, 1)
+    late = [(_links(topo, left, core), 0, S.gotL, T.acc[:, 0:HALO], w0, T.hL[:]),
+            (_links(topo, right, core), 1, S.gotR, T.acc[:, P - HALO:P], w2, T.hR[:])]
+    late.sort(key=lambda t: (t[0], t[1]))
+    for i, (_, _, sem, out, wt, halo) in enumerate(late):
+        te.wait_ge(sem, ENG)
+        te.matmul(out, wt, halo, False, i == 1).then_inc(S.mm, 1)
+
+    g.vector.wait_ge(S.mm, 5)
+    g.vector.tensor_copy(T.ys[:], T.acc[:]).then_inc(S.cp, 1)
+    g.sync.wait_ge(S.cp, 1)
+    g.sync.dma_start(T.y[:], T.ys[:]).then_inc(S.st, 16)
+    g.sync.wait_ge(S.st, 16)
+
+    g.wait_ge(S.sent, 2 * ENG)

@@ -1,26 +1,25 @@
-from concourse.bass import DstId, RemoteDMATransfer
+from concourse.mybir import AluOpType
 
 P = 128
 HALO = 8
 ENG = 4
+BANK = 512
 
 SCRATCH = {
+    "xe": ("sbuf", [P, 2 * HALO], "float32"),
     "xs": ("sbuf", [P, P], "float32"),
     "ws": ("sbuf", [P, 3 * P], "float32"),
     "hL": ("sbuf", [P, HALO], "float32"),
     "hR": ("sbuf", [P, HALO], "float32"),
     "ys": ("sbuf", [P, P], "float32"),
-    "acc": ("psum", [P, P], "float32"),
+    "yL": ("sbuf", [P, HALO], "float32"),
+    "yR": ("sbuf", [P, HALO], "float32"),
+    "acc": ("psum", [P, BANK], "float32"),
+    "accL": ("psum", [P, BANK], "float32"),
+    "accR": ("psum", [P, BANK], "float32"),
 }
-SEMAPHORES = ["xl", "wl", "sent", "gotL", "gotR", "mm", "cp", "st"]
-
-
-def _links(topo, a, b):
-    if topo.same_plane(a, b):
-        return 1
-    if topo.rack(topo.host(a)) != topo.rack(topo.host(b)) and topo.chip(a) == topo.chip(b):
-        return 1
-    return 2
+SEMAPHORES = ["eL", "eR", "xl", "wl0", "wl1", "wl2", "sent", "gotL", "gotR", "mm", "cp", "mL", "mR", "aL", "aR", "st",
+              "stL", "stR"]
 
 
 def rank_program(g, core, T, topo):
@@ -28,44 +27,62 @@ def rank_program(g, core, T, topo):
     if rank is None:
         return
     n = len(T.cores)
-    left, right = T.cores[(rank - 1) % n], T.cores[(rank + 1) % n]
     S = T.sem
-
-    g.sync.dma_start(T.xs[:], T.x[:]).then_inc(S.xl, 16)
-    g.sync.dma_start(T.ws[:], T.w[:]).then_inc(S.wl, 16)
-
-    both = topo.mask(core, left) & topo.mask(core, right)
-    engines = [e for e in range(16) if (both >> e) & 1]
-    m_left = sum(1 << e for e in engines[0:ENG])
-    m_right = sum(1 << e for e in engines[ENG:2 * ENG])
-    rid_l, pid_l = topo.addr(left, core)
-    rid_r, pid_r = topo.addr(right, core)
-    g.wait_ge(S.xl, 16)
-    g.remote_dma_fused([
-        RemoteDMATransfer(dst_ids=[DstId(rid=rid_l, pnc=pid_l)], dma_engine_mask=m_left, remote_sem=S.gotR,
-                          src=T.xs[:, 0:HALO], dst=T.hR[:]),
-        RemoteDMATransfer(dst_ids=[DstId(rid=rid_r, pnc=pid_r)], dma_engine_mask=m_right, remote_sem=S.gotL,
-                          src=T.xs[:, P - HALO:P], dst=T.hL[:]),
-    ], local_sem=S.sent)
-
     w0, w1, w2 = T.ws[:, 0:P], T.ws[:, P:2 * P], T.ws[:, 2 * P:3 * P]
+
+    sides = [
+        dict(peer=T.cores[(rank - 1) % n], xcols=T.x[:, 0:HALO], mine=T.xe[:, 0:HALO], loaded=S.eL,
+             there=T.hR[:], tell=S.gotR,
+             got=S.gotL, halo=T.hL[:], tile=w0, ps=T.accL[:, 0:HALO], done=S.mL, own=T.ys[:, 0:HALO], fin=T.yL[:],
+             added=S.aL, ycols=T.y[:, 0:HALO], stored=S.stL),
+        dict(peer=T.cores[(rank + 1) % n], xcols=T.x[:, P - HALO:P], mine=T.xe[:, HALO:2 * HALO], loaded=S.eR,
+             there=T.hL[:], tell=S.gotL,
+             got=S.gotR, halo=T.hR[:], tile=w2, ps=T.accR[:, 0:HALO], done=S.mR, own=T.ys[:, P - HALO:P], fin=T.yR[:],
+             added=S.aR, ycols=T.y[:, P - HALO:P], stored=S.stR),
+    ]
+    my_rack = topo.rack(topo.host(core))
+    sides.sort(key=lambda s: 1 if topo.rack(topo.host(s["peer"])) == my_rack else 0)
+
+    for q, s in zip((g.sync, g.scalar), sides):
+        q.dma_start(s["mine"], s["xcols"]).then_inc(s["loaded"], 16)
+    g.sync.dma_start(T.xs[:], T.x[:]).then_inc(S.xl, 16)
+    for i in (1, 0, 2):
+        g.sync.dma_start(T.ws[:, i * P:(i + 1) * P], T.w[:, i * P:(i + 1) * P]).then_inc(S["wl%d" % i], 16)
+
+    both = topo.mask(core, sides[0]["peer"]) & topo.mask(core, sides[1]["peer"])
+    engines = [e for e in range(16) if (both >> e) & 1]
+    for k, s in enumerate(sides):
+        rid, pid = topo.addr(s["peer"], core)
+        mask = sum(1 << e for e in engines[k * ENG:(k + 1) * ENG])
+        g.wait_ge(s["loaded"], 16)
+        g.remote_dma(s["there"], s["mine"], s["tell"], S.sent, pid, rid, mask)
+
     te = g.tensor
     te.wait_ge(S.xl, 16)
-    te.wait_ge(S.wl, 16)
+    te.wait_ge(S.wl1, 16)
     te.matmul(T.acc[:, 0:P], w1, T.xs[:, 0:P], True, False).then_inc(S.mm, 1)
+    te.wait_ge(S.wl0, 16)
     te.matmul(T.acc[:, HALO:P], w0, T.xs[:, 0:P - HALO], False, False).then_inc(S.mm, 1)
-    te.matmul(T.acc[:, 0:P - HALO], w2, T.xs[:, HALO:P], False, False).then_inc(S.mm, 1)
-    late = [(_links(topo, left, core), 0, S.gotL, T.acc[:, 0:HALO], w0, T.hL[:]),
-            (_links(topo, right, core), 1, S.gotR, T.acc[:, P - HALO:P], w2, T.hR[:])]
-    late.sort(key=lambda t: (t[0], t[1]))
-    for i, (_, _, sem, out, wt, halo) in enumerate(late):
-        te.wait_ge(sem, ENG)
-        te.matmul(out, wt, halo, False, i == 1).then_inc(S.mm, 1)
+    te.wait_ge(S.wl2, 16)
+    te.matmul(T.acc[:, 0:P - HALO], w2, T.xs[:, HALO:P], False, True).then_inc(S.mm, 1)
+    for s in sides:
+        te.wait_ge(s["got"], ENG)
+        te.matmul(s["ps"], s["tile"], s["halo"], True, True).then_inc(s["done"], 1)
 
-    g.vector.wait_ge(S.mm, 5)
-    g.vector.tensor_copy(T.ys[:], T.acc[:]).then_inc(S.cp, 1)
+    ve = g.vector
+    ve.wait_ge(S.mm, 3)
+    ve.tensor_copy(T.ys[:], T.acc[:, 0:P]).then_inc(S.cp, 1)
+    ve.wait_ge(S.cp, 1)
+    for s in sides:
+        ve.wait_ge(s["done"], 1)
+        ve.tensor_tensor(s["fin"], s["ps"], s["own"], AluOpType.add).then_inc(s["added"], 1)
+
     g.sync.wait_ge(S.cp, 1)
-    g.sync.dma_start(T.y[:], T.ys[:]).then_inc(S.st, 16)
+    g.sync.dma_start(T.y[:, HALO:P - HALO], T.ys[:, HALO:P - HALO]).then_inc(S.st, 16)
+    for q, s in zip((g.scalar, g.sync), sides):
+        q.wait_ge(s["added"], 1)
+        q.dma_start(s["ycols"], s["fin"]).then_inc(s["stored"], 16)
+        q.wait_ge(s["stored"], 16)
     g.sync.wait_ge(S.st, 16)
 
     g.wait_ge(S.sent, 2 * ENG)

from concourse.mybir import AluOpType

P = 128
HALO = 8
ENG = 4
BANK = 512

SCRATCH = {
    "xe": ("sbuf", [P, 2 * HALO], "float32"),
    "xs": ("sbuf", [P, P], "float32"),
    "ws": ("sbuf", [P, 3 * P], "float32"),
    "hL": ("sbuf", [P, HALO], "float32"),
    "hR": ("sbuf", [P, HALO], "float32"),
    "ys": ("sbuf", [P, P], "float32"),
    "yL": ("sbuf", [P, HALO], "float32"),
    "yR": ("sbuf", [P, HALO], "float32"),
    "acc": ("psum", [P, BANK], "float32"),
    "accL": ("psum", [P, BANK], "float32"),
    "accR": ("psum", [P, BANK], "float32"),
}
SEMAPHORES = ["eL", "eR", "xl", "wl0", "wl1", "wl2", "sent", "gotL", "gotR", "mm", "cp", "mL", "mR", "aL", "aR", "st",
              "stL", "stR"]


def rank_program(g, core, T, topo):
    rank = T.rank_of(core)
    if rank is None:
        return
    n = len(T.cores)
    S = T.sem
    w0, w1, w2 = T.ws[:, 0:P], T.ws[:, P:2 * P], T.ws[:, 2 * P:3 * P]

    sides = [
        dict(peer=T.cores[(rank - 1) % n], xcols=T.x[:, 0:HALO], mine=T.xe[:, 0:HALO], loaded=S.eL,
             there=T.hR[:], tell=S.gotR,
             got=S.gotL, halo=T.hL[:], tile=w0, ps=T.accL[:, 0:HALO], done=S.mL, own=T.ys[:, 0:HALO], fin=T.yL[:],
             added=S.aL, ycols=T.y[:, 0:HALO], stored=S.stL),
        dict(peer=T.cores[(rank + 1) % n], xcols=T.x[:, P - HALO:P], mine=T.xe[:, HALO:2 * HALO], loaded=S.eR,
             there=T.hL[:], tell=S.gotL,
             got=S.gotR, halo=T.hR[:], tile=w2, ps=T.accR[:, 0:HALO], done=S.mR, own=T.ys[:, P - HALO:P], fin=T.yR[:],
             added=S.aR, ycols=T.y[:, P - HALO:P], stored=S.stR),
    ]
    my_rack = topo.rack(topo.host(core))
    sides.sort(key=lambda s: 1 if topo.rack(topo.host(s["peer"])) == my_rack else 0)

    for q, s in zip((g.sync, g.scalar), sides):
        q.dma_start(s["mine"], s["xcols"]).then_inc(s["loaded"], 16)
    g.sync.dma_start(T.xs[:], T.x[:]).then_inc(S.xl, 16)
    for i in (1, 0, 2):
        g.sync.dma_start(T.ws[:, i * P:(i + 1) * P], T.w[:, i * P:(i + 1) * P]).then_inc(S["wl%d" % i], 16)

    both = topo.mask(core, sides[0]["peer"]) & topo.mask(core, sides[1]["peer"])
    engines = [e for e in range(16) if (both >> e) & 1]
    for k, s in enumerate(sides):
        rid, pid = topo.addr(s["peer"], core)
        mask = sum(1 << e for e in engines[k * ENG:(k + 1) * ENG])
        g.wait_ge(s["loaded"], 16)
        g.remote_dma(s["there"], s["mine"], s["tell"], S.sent, pid, rid, mask)

    te = g.tensor
    te.wait_ge(S.xl, 16)
    te.wait_ge(S.wl1, 16)
    te.matmul(T.acc[:, 0:P], w1, T.xs[:, 0:P], True, False).then_inc(S.mm, 1)
    te.wait_ge(S.wl0, 16)
    te.matmul(T.acc[:, HALO:P], w0, T.xs[:, 0:P - HALO], False, False).then_inc(S.mm, 1)
    te.wait_ge(S.wl2, 16)
    te.matmul(T.acc[:, 0:P - HALO], w2, T.xs[:, HALO:P], False, True).then_inc(S.mm, 1)
    for s in sides:
        te.wait_ge(s["got"], ENG)
        te.matmul(s["ps"], s["tile"], s["halo"], True, True).then_inc(s["done"], 1)

    ve = g.vector
    ve.wait_ge(S.mm, 3)
    ve.tensor_copy(T.ys[:], T.acc[:, 0:P]).then_inc(S.cp, 1)
    ve.wait_ge(S.cp, 1)
    for s in sides:
        ve.wait_ge(s["done"], 1)
        ve.tensor_tensor(s["fin"], s["ps"], s["own"], AluOpType.add).then_inc(s["added"], 1)

    g.sync.wait_ge(S.cp, 1)
    g.sync.dma_start(T.y[:, HALO:P - HALO], T.ys[:, HALO:P - HALO]).then_inc(S.st, 16)
    for q, s in zip((g.scalar, g.sync), sides):
        q.wait_ge(s["added"], 1)
        q.dma_start(s["ycols"], s["fin"]).then_inc(s["stored"], 16)
        q.wait_ge(s["stored"], 16)
    g.sync.wait_ge(S.st, 16)

    g.wait_ge(S.sent, 2 * ENG)
